import numpy as np
import ml_dtypes


def mxq(x, axis, fmt="e4m3"):
    dtype, down = {"e4m3": (ml_dtypes.float8_e4m3fn, 7), "e5m2": (ml_dtypes.float8_e5m2, 14)}[fmt]
    v = np.moveaxis(np.asarray(x, np.float32).astype(ml_dtypes.bfloat16).astype(np.float64), axis, -1)
    blocks = v.reshape(v.shape[:-1] + (-1, 32))
    amax = np.abs(blocks).max(-1, keepdims=True)
    byte = np.maximum(np.where(amax > 0, np.frexp(amax)[1] - 1 + 127, 0) - down, 1)
    scale = np.exp2(byte - 127.0)
    codes = (blocks / scale).astype(np.float32).astype(dtype).astype(np.float64)
    return np.moveaxis((codes * scale).reshape(v.shape), -1, axis)


WIDE = False


def mx_kscale(k):
    if not WIDE:
        return np.ones(k)
    levels = np.array([30, -30])
    if k % 512:
        return np.exp2(np.random.permutation(np.resize(levels, k // 32))).repeat(32)
    a = np.empty((k // 512, 16))
    for p in range(k // 512):
        a[p, :8] = np.random.permutation(np.resize(levels, 8))
        for g in range(8):
            far = levels[np.abs(levels - a[p, g]) >= 10]
            a[p, g + 8] = far[np.random.randint(len(far))]
    return np.exp2(a.ravel()).repeat(32)


def f64(x):
    return np.asarray(x).astype(np.float64)


def striped(idx):
    return np.tile(np.asarray(idx).reshape(-1, 16).T, (8, 1)).astype(np.uint16)


def unstriped(offs):
    return offs[:16].T.reshape(-1).astype(np.int64)


def striped8(idx):
    return np.asarray(idx).reshape(8, -1, 16).transpose(0, 2, 1).reshape(128, -1).astype(np.uint16)


def unstriped8(offs):
    return offs.reshape(8, 16, -1).transpose(0, 2, 1).reshape(8, -1).astype(np.int64)


def pick8(x, idx, run):
    r = np.arange(len(x))
    return x[r[:, None], idx[r % (8 * run) // run]]


E2M1 = np.array([0.0, 0.5, 1.0, 1.5, 2.0, 3.0, 4.0, 6.0, -0.0, -0.5, -1.0, -1.5, -2.0, -3.0, -4.0, -6.0])


def pack_weight(w, fmt):
    k, n = w.shape
    w = f64(np.asarray(w, np.float32).astype(ml_dtypes.bfloat16)).reshape(k // 32, 32, n)
    amax = np.abs(w).max(1)
    if fmt in ("e4m3", "e5m2"):
        byte = np.frexp(amax)[1] - 1 + 127 - (7 if fmt == "e4m3" else 14)
    else:
        mant, ex = np.frexp(amax / 6.0)
        byte = np.where(mant > 0.5, ex, ex - 1) + 127
    byte = np.clip(np.where(amax > 0, byte, 1), 1, 254)
    scaled = (w * np.exp2(127.0 - byte)[:, None, :]).reshape(k, n).astype(np.float32)
    by_word = np.ascontiguousarray(scaled.reshape(k // 512, 128, 4, n).transpose(0, 1, 3, 2))
    if fmt in ("e4m3", "e5m2"):
        words = by_word.astype(ml_dtypes.float8_e4m3fn if fmt == "e4m3" else ml_dtypes.float8_e5m2).view(np.uint8)
    else:
        c = by_word.astype(ml_dtypes.float4_e2m1fn).view(np.uint8) & 0xF
        words = (c[..., 0::2] | (c[..., 1::2] << 4)).reshape(k // 512, 128, 2 * n)
    return np.ascontiguousarray(words), np.ascontiguousarray(byte.astype(np.uint8).reshape(k // 512, 16, n))


def unpack_weight(words, scales, fmt):
    g, _, n = scales.shape
    words = np.ascontiguousarray(words).reshape(g, 128, n, -1)
    if fmt in ("e4m3", "e5m2"):
        vals = words.view(ml_dtypes.float8_e4m3fn if fmt == "e4m3" else ml_dtypes.float8_e5m2).astype(np.float64)
    else:
        nib = np.empty((g, 128, n, 4), np.uint8)
        nib[..., 0::2] = words & 0xF
        nib[..., 1::2] = words >> 4
        vals = E2M1[nib]
    vals = vals * np.repeat(np.exp2(scales.astype(np.float64) - 127.0), 8, axis=1)[..., None]
    return vals.transpose(0, 1, 3, 2).reshape(g * 512, n)


K, T, J, R, C, D, O, N, E = 512, 1024, 256, 512, 512, 512, 256, 256, 512


def setup_inputs():
    n = np.random.standard_normal
    idx = np.random.permutation(T)[:J]
    idx2 = np.stack([np.random.permutation(C)[:J] for _ in range(8)])
    idx3 = np.stack([np.random.permutation(D)[:J] for _ in range(8)])
    idx4 = np.random.permutation(C)[:O]
    idx5 = np.random.permutation(D)[:O]
    idx6 = np.stack([np.random.permutation(E)[:O] for _ in range(8)])
    idx7 = np.random.permutation(E)[:O]
    fk = mx_kscale(K)
    fr = mx_kscale(R)
    xtp = pack_weight(n((K, T)) / fk[:, None], "e2m1")
    wp = pack_weight(n((K, R)) * 1 / np.sqrt(K) * fk[:, None] * fr, "e4m3")
    w2p = pack_weight(n((K, R)) * 1 / np.sqrt(K) * fk[:, None] * fr, "e5m2")
    wbp = pack_weight(n((R, N)) * 1 / np.sqrt(R) / fr[:, None], "e2m1")
    return {
        "xt_words": xtp[0],
        "xt_scales": xtp[1],
        "w_words": wp[0],
        "w_scales": wp[1],
        "w2_words": w2p[0],
        "w2_scales": w2p[1],
        "sa": (np.random.uniform(0.5, 1.6, (R, 1))).astype(np.float32),
        "sb": (np.random.uniform(0.5, 1.6, (R, 1))).astype(np.float32),
        "wb_words": wbp[0],
        "wb_scales": wbp[1],
        "offs": striped(idx),
        "offs2": striped8(idx2),
        "offs3": striped8(idx3),
        "offs4": striped(idx4),
        "offs5": striped(idx5),
        "offs6": striped8(idx6),
        "offs7": striped(idx7),
    }


def reference(xt_words, xt_scales, w_words, w_scales, w2_words, w2_scales, sa, sb, wb_words, wb_scales, offs, offs2, offs3, offs4, offs5, offs6, offs7):
    idx = unstriped(offs)
    idx2 = unstriped8(offs2)
    idx3 = unstriped8(offs3)
    idx4 = unstriped(offs4)
    idx5 = unstriped(offs5)
    idx6 = unstriped8(offs6)
    idx7 = unstriped(offs7)
    xtu = unpack_weight(xt_words, xt_scales, "e2m1")
    wu = unpack_weight(w_words, w_scales, "e4m3")
    w2u = unpack_weight(w2_words, w2_scales, "e5m2")
    wbu = unpack_weight(wb_words, wb_scales, "e2m1")
    xtidxg = xtu[:, idx]
    a = wu.T @ xtidxg
    b = w2u.T @ xtidxg
    pw = np.zeros((R, C))
    pw[np.arange(R)[:, None], idx2[np.arange(R) % 512 // 64]] = a
    pv = np.zeros((R, D))
    pv[np.arange(R)[:, None], idx3[np.arange(R) % 512 // 64]] = b
    hid = np.abs(pw[:, idx4] * f64(sa) - pv[:, idx5] * f64(sb))
    hidq = mxq(hid, 0, "e5m2")
    p = wbu.T @ hidq
    pa = np.zeros((N, E))
    pa[np.arange(N)[:, None], idx6[np.arange(N) % 128 // 16]] = p
    pb = np.zeros((N, E))
    pb[:, idx7] = p
    y = pa + pb
    return y

@@ -1,0 +1,195 @@
+from contextlib import ExitStack
+
+import concourse.mybir as mybir
+
+K, T, J, R, C, O, N, E = 512, 1024, 256, 512, 512, 256, 256, 512
+FLOPS = 2 * K * R * J * 2 + 2 * R * N * O
+
+F32 = mybir.dt.float32
+BF16 = mybir.dt.bfloat16
+I32 = mybir.dt.int32
+U32 = mybir.dt.uint32
+U16 = mybir.dt.uint16
+U8 = mybir.dt.uint8
+E4M3 = mybir.dt.float8_e4m3fn_x4
+E5M2 = mybir.dt.float8_e5m2_x4
+E2M1 = mybir.dt.float4_e2m1fn_x4
+ALU = mybir.AluOpType
+COPY = mybir.ActivationFunctionType.Copy
+
+P = 128
+PACK = 4
+HALF = 128
+
+
+def tile_list_twoownboards_twow_one_owntwopages_kernel(
+    tc, xt_words, xt_scales, w_words, w_scales, w2_words, w2_scales, sa, sb, wb_words, wb_scales,
+    offs, offs2, offs3, offs4, offs5, offs6, offs7, out
+):
+    nc = tc.nc
+    with ExitStack() as ctx:
+        held = ctx.enter_context(tc.tile_pool(name="held", bufs=1))
+        psum_ab = ctx.enter_context(tc.psum_pool(name="psum_ab", bufs=6))
+        psum_p = ctx.enter_context(tc.psum_pool(name="psum_p", bufs=2))
+
+        def sbuf(shape, dtype, name, tag=None):
+            return held.tile(shape, dtype, name=name, tag=tag or name, align_bytes=64)
+
+        def load_list(src, name):
+            lst = held.tile([P, J // 16], U16, name=name)
+            nc.sync.dma_start(lst[:], src)
+            return lst
+
+        def load_plane(plane, scales):
+            for q in range(4):
+                nc.sync.dma_start(plane[32 * q : 32 * q + 4, :].bitcast(I32), scales[0, 4 * q : 4 * q + 4, :].bitcast(I32))
+
+        def half_of(lst, h):
+            return lst[:, h * HALF // 16 : (h + 1) * HALF // 16]
+
+        x_plane = sbuf([P, T], U8, "x_plane")
+        w_plane = sbuf([P, R], U8, "w_plane")
+        w2_plane = sbuf([P, R], U8, "w2_plane")
+        wb_plane = sbuf([P, N], U8, "wb_plane")
+        for plane in (x_plane, w_plane, w2_plane, wb_plane):
+            nc.vector.memset(plane[:].bitcast(I32), 0)
+
+        x_rows = sbuf([4, 4, T // 4], I32, "x_rows")
+        nc.sync.dma_start(x_rows[:], xt_scales[0].bitcast(I32).rearrange("(q r) c -> r q c", r=4))
+        w_rows = sbuf([4, 4, R // 4], I32, "w_rows")
+        nc.sync.dma_start(w_rows[:], w_scales[0].bitcast(I32).rearrange("(q r) c -> r q c", r=4))
+        x_words = sbuf([P, T], U16, "x_words")
+        nc.sync.dma_start(x_words[:].bitcast(I32), xt_words[0].bitcast(I32))
+        list1 = load_list(offs, "list1")
+        w_raw = sbuf([P, R], I32, "w_raw")
+        nc.sync.dma_start(w_raw[:], w_words[0].rearrange("p n t -> p (n t)").bitcast(I32))
+        list2 = load_list(offs2, "list2")
+        w2_raw = sbuf([P, R], I32, "w2_raw")
+        nc.sync.dma_start(w2_raw[:], w2_words[0].rearrange("p n t -> p (n t)").bitcast(I32))
+        load_plane(w2_plane, w2_scales)
+        list3 = load_list(offs3, "list3")
+        wb_codes = sbuf([P, 2 * N], U8, "wb_codes")
+        nc.sync.dma_start(wb_codes[:].bitcast(I32), wb_words[0].bitcast(I32))
+        load_plane(wb_plane, wb_scales)
+        list6 = load_list(offs6, "list6")
+        list7 = load_list(offs7, "list7")
+        sa_t = sbuf([P, PACK], F32, "sa_t")
+        nc.sync.dma_start(sa_t[:], sa.rearrange("(p t) o -> p (t o)", t=PACK))
+        sb_t = sbuf([P, PACK], F32, "sb_t")
+        nc.sync.dma_start(sb_t[:], sb.rearrange("(p t) o -> p (t o)", t=PACK))
+        list5 = load_list(offs5, "list5")
+        list4 = load_list(offs4, "list4")
+
+        for q in range(4):
+            nc.vector.tensor_copy(x_plane[32 * q : 32 * q + 4, :].bitcast(I32), x_rows[:, q, :])
+        for q in range(4):
+            nc.vector.tensor_copy(w_plane[32 * q : 32 * q + 4, :].bitcast(I32), w_rows[:, q, :])
+        w_scale0 = sbuf([P, P], U8, "w_scale0")
+        w_plane_dealt = w_plane[:].rearrange("p (m t) -> p t m", t=PACK)
+        nc.vector.tensor_copy(w_scale0[:], w_plane_dealt[:, 0, :])
+
+        xg_words = sbuf([P, J], U16, "xg_words")
+        xg_plane = sbuf([P, J], U8, "xg_plane")
+        w_codes0 = sbuf([P, P], I32, "w_codes0")
+        w2_codes = sbuf([P, PACK, P], I32, "w2_codes")
+        w2_scale = sbuf([P, PACK, P], U8, "w2_scale")
+
+        def gather_x(h):
+            cols = slice(h * HALF, (h + 1) * HALF)
+            nc.vector.tensor_copy(xg_words[:, cols], x_words[:].indirect(half_of(list1, h)))
+            nc.vector.tensor_copy(xg_plane[:, cols], x_plane[:].indirect(half_of(list1, h)))
+
+        def deal(codes, raw, t):
+            nc.vector.tensor_copy(codes[:, t, :], raw[:].rearrange("p (m t) -> p t m", t=PACK)[:, t, :])
+
+        def board(name, tag=None):
+            tile_ = sbuf([P, C], F32, name, tag)
+            nc.vector.memset(tile_[:], 0.0)
+            return tile_
+
+        a_sb = [sbuf([P, J], F32, "a_sb%d" % t) for t in range(PACK)]
+        b_sb = [sbuf([P, J], F32, "b_sb%d" % t) for t in range(PACK)]
+
+        def first_stage(codes, scale, fmt, staged, dest, lst, j0, j1):
+            acc = psum_ab.tile([P, J], F32, name="acc")
+            nc.tensor.matmul_mx(
+                out=acc[:, 0 : j1 - j0],
+                lhsT=codes.bitcast(fmt),
+                lhsT_scale=scale,
+                rhs=xg_words[:, j0:j1].bitcast(E2M1),
+                rhs_scale=xg_plane[:, j0:j1],
+                start=True,
+                stop=True,
+            )
+            if j1 == HALF:
+                nc.scalar.copy(staged[:, j0:j1], acc[:, 0 : j1 - j0])
+            else:
+                nc.vector.tensor_copy(staged[:, j0:j1], acc[:, 0 : j1 - j0])
+            nc.scalar.activation(dest[:].indirect(lst[:, j0 // 16 : j1 // 16]), staged[:, j0:j1], COPY)
+
+        pw = [board("pw0"), board("pw1")]
+        gather_x(0)
+        nc.scalar.copy(w_codes0[:].bitcast(U32), w_raw[:].bitcast(U32).rearrange("p (m t) -> p t m", t=PACK)[:, 0, :])
+        gather_x(1)
+        first_stage(w_codes0[:], w_scale0[:], E4M3, a_sb[0], pw[0], list2, 0, HALF)
+        first_stage(w_codes0[:], w_scale0[:], E4M3, a_sb[0], pw[0], list2, HALF, J)
+        w_scale = sbuf([P, PACK, P], U8, "w_scale", "x_words")
+        w_codes = sbuf([P, PACK, P], I32, "w_codes", "x_plane")
+        for t in range(1, PACK):
+            nc.vector.tensor_copy(w_scale[:, t, :], w_plane_dealt[:, t, :])
+            deal(w_codes, w_raw, t)
+        for t in range(1, PACK):
+            if t >= 2:
+                pw.append(board("pw%d" % t, ("w_plane", "w_raw")[t - 2]))
+            first_stage(w_codes[:, t, :], w_scale[:, t, :], E4M3, a_sb[t], pw[t], list2, 0, J)
+        nc.vector.tensor_copy(w2_scale[:], w2_plane[:].rearrange("p (m t) -> p t m", t=PACK))
+        for t in range(PACK):
+            deal(w2_codes, w2_raw, t)
+        pv = []
+        for t in range(PACK):
+            pv.append(board("pv%d" % t, ("x_plane", "x_words", "w2_plane", "w2_raw")[t]))
+            first_stage(w2_codes[:, t, :], w2_scale[:, t, :], E5M2, b_sb[t], pv[t], list3, 0, J)
+        pa = [board("pa0", "w2_codes"), board("pa1", "w2_scale")]
+        pb = [board("pb0", "xg_words"), board("pb1", "xg_plane")]
+
+        p_sb = []
+        for h in range(2):
+            picked = sbuf([P, 2, PACK, HALF], F32, "picked%d" % h, ("picked0", "b_sb3")[h])
+            ga, gb = picked[:, 0], picked[:, 1]
+            diff = sbuf([P, PACK, HALF], F32, "diff%d" % h)
+            for t in range(PACK):
+                nc.scalar.activation(ga[:, t, :], pw[t][:].indirect(half_of(list4, h)), COPY, scale=sa_t[:, t : t + 1])
+                nc.scalar.activation(gb[:, t, :], pv[t][:].indirect(half_of(list5, h)), COPY, scale=sb_t[:, t : t + 1])
+                nc.vector.tensor_tensor(diff[:, t, :], ga[:, t, :], gb[:, t, :], ALU.subtract)
+            hid = sbuf([P, HALF, PACK], BF16, "hid%d" % h)
+            woven = diff[:].rearrange("p t o -> p o t")
+            nc.vector.scalar_tensor_tensor(hid[:], woven, -1.0, woven, ALU.mult, ALU.max)
+            hid_codes = sbuf([P, HALF], I32, "hid_codes%d" % h)
+            hid_scale = sbuf([P, HALF], U8, "hid_scale%d" % h)
+            nc.vector.quantize_mx(hid_codes[:].bitcast(E5M2), hid_scale[:], hid[:].rearrange("p o t -> p (o t)"))
+            acc_p = psum_p.tile([P, 2, HALF], F32, name="acc_p")
+            for g in range(2):
+                nc.tensor.matmul_mx(
+                    out=acc_p[:, g, :],
+                    lhsT=wb_codes[:, 2 * P * g : 2 * P * (g + 1)].bitcast(E2M1),
+                    lhsT_scale=wb_plane[:, P * g : P * (g + 1)],
+                    rhs=hid_codes[:].bitcast(E5M2),
+                    rhs_scale=hid_scale[:],
+                    start=True,
+                    stop=True,
+                )
+            staged = sbuf([P, 2, HALF], F32, "p_sb%d" % h)
+            if h == 0:
+                nc.vector.tensor_copy(staged[:], acc_p[:])
+            else:
+                nc.scalar.copy(staged[:], acc_p[:])
+            p_sb.append(staged)
+
+        for h in range(2):
+            for g in range(2):
+                nc.scalar.activation(pa[g][:].indirect(half_of(list6, h)), p_sb[h][:, g, :], COPY)
+                nc.vector.tensor_copy(pb[g][:].indirect(half_of(list7, h)), p_sb[h][:, g, :])
+        for g in range(2):
+            total = sbuf([P, E], F32, "total%d" % g)
+            nc.vector.tensor_tensor(total[:], pa[g][:], pb[g][:], ALU.add)
+            nc.sync.dma_start(out[P * g : P * (g + 1), :], total[:])

@@ -90,9 +90,8 @@ def tile_list_twoownboards_twow_one_owntwopages_kernel(
 
         xg_words = sbuf([P, J], U16, "xg_words")
         xg_plane = sbuf([P, J], U8, "xg_plane")
-        w_codes0 = sbuf([P, P], I32, "w_codes0")
-        w2_codes = sbuf([P, PACK, P], I32, "w2_codes")
-        w2_scale = sbuf([P, PACK, P], U8, "w2_scale")
+        w_codes0 = sbuf([P, P], U32, "w_codes0")
+        w_codes = sbuf([P, PACK, P], U32, "w_codes")
 
         def gather_x(h):
             cols = slice(h * HALF, (h + 1) * HALF)
@@ -110,7 +109,7 @@ def tile_list_twoownboards_twow_one_owntwopages_kernel(
         a_sb = [sbuf([P, J], F32, "a_sb%d" % t) for t in range(PACK)]
         b_sb = [sbuf([P, J], F32, "b_sb%d" % t) for t in range(PACK)]
 
-        def first_stage(codes, scale, fmt, staged, dest, lst, j0, j1):
+        def first_product(codes, scale, fmt, j0, j1):
             acc = psum_ab.tile([P, J], F32, name="acc")
             nc.tensor.matmul_mx(
                 out=acc[:, 0 : j1 - j0],
@@ -121,46 +120,48 @@ def tile_list_twoownboards_twow_one_owntwopages_kernel(
                 start=True,
                 stop=True,
             )
+            return acc
+
+        def put_first(acc, staged, dest, lst, j0, j1):
             if j1 == HALF:
                 nc.scalar.copy(staged[:, j0:j1], acc[:, 0 : j1 - j0])
             else:
                 nc.vector.tensor_copy(staged[:, j0:j1], acc[:, 0 : j1 - j0])
             nc.scalar.activation(dest[:].indirect(lst[:, j0 // 16 : j1 // 16]), staged[:, j0:j1], COPY)
 
-        pw = [board("pw0"), board("pw1")]
+        pw = [board("pw%d" % t) for t in range(PACK)]
         gather_x(0)
-        nc.scalar.copy(w_codes0[:].bitcast(U32), w_raw[:].bitcast(U32).rearrange("p (m t) -> p t m", t=PACK)[:, 0, :])
+        w_raw_dealt = w_raw[:].bitcast(U32).rearrange("p (m t) -> p t m", t=PACK)
+        nc.scalar.copy(w_codes0[:], w_raw_dealt[:, 0, :])
+        nc.scalar.copy(w_codes[:, 1:PACK, :], w_raw_dealt[:, 1:PACK, :])
         gather_x(1)
-        first_stage(w_codes0[:], w_scale0[:], E4M3, a_sb[0], pw[0], list2, 0, HALF)
-        first_stage(w_codes0[:], w_scale0[:], E4M3, a_sb[0], pw[0], list2, HALF, J)
+        put_first(first_product(w_codes0[:], w_scale0[:], E4M3, 0, HALF), a_sb[0], pw[0], list2, 0, HALF)
+        put_first(first_product(w_codes0[:], w_scale0[:], E4M3, HALF, J), a_sb[0], pw[0], list2, HALF, J)
         w_scale = sbuf([P, PACK, P], U8, "w_scale", "x_words")
-        w_codes = sbuf([P, PACK, P], I32, "w_codes", "x_plane")
         for t in range(1, PACK):
             nc.vector.tensor_copy(w_scale[:, t, :], w_plane_dealt[:, t, :])
-            deal(w_codes, w_raw, t)
+        accs = {t: first_product(w_codes[:, t, :], w_scale[:, t, :], E4M3, 0, J) for t in range(1, PACK)}
         for t in range(1, PACK):
-            if t >= 2:
-                pw.append(board("pw%d" % t, ("w_plane", "w_raw")[t - 2]))
-            first_stage(w_codes[:, t, :], w_scale[:, t, :], E4M3, a_sb[t], pw[t], list2, 0, J)
+            put_first(accs[t], a_sb[t], pw[t], list2, 0, J)
+        w2_codes = sbuf([P, PACK, P], I32, "w2_codes", "w_codes")
+        w2_scale = sbuf([P, PACK, P], U8, "w2_scale", "x_words")
         nc.vector.tensor_copy(w2_scale[:], w2_plane[:].rearrange("p (m t) -> p t m", t=PACK))
         for t in range(PACK):
             deal(w2_codes, w2_raw, t)
+        accs = {t: first_product(w2_codes[:, t, :], w2_scale[:, t, :], E5M2, 0, J) for t in range(PACK)}
         pv = []
         for t in range(PACK):
-            pv.append(board("pv%d" % t, ("x_plane", "x_words", "w2_plane", "w2_raw")[t]))
-            first_stage(w2_codes[:, t, :], w2_scale[:, t, :], E5M2, b_sb[t], pv[t], list3, 0, J)
-        pa = [board("pa0", "w2_codes"), board("pa1", "w2_scale")]
-        pb = [board("pb0", "xg_words"), board("pb1", "xg_plane")]
+            pv.append(board("pv%d" % t, ("w2_plane", "w2_raw", "w_codes", "x_words")[t]))
+            put_first(accs[t], b_sb[t], pv[t], list3, 0, J)
+        pa = [board("pa0", "xg_words"), board("pa1", "xg_plane")]
+        pb = [board("pb0", "b_sb0"), board("pb1", "b_sb1")]
 
-        p_sb = []
-        for h in range(2):
-            picked = sbuf([P, 2, PACK, HALF], F32, "picked%d" % h, ("picked0", "b_sb3")[h])
-            ga, gb = picked[:, 0], picked[:, 1]
-            diff = sbuf([P, PACK, HALF], F32, "diff%d" % h)
-            for t in range(PACK):
-                nc.scalar.activation(ga[:, t, :], pw[t][:].indirect(half_of(list4, h)), COPY, scale=sa_t[:, t : t + 1])
-                nc.scalar.activation(gb[:, t, :], pv[t][:].indirect(half_of(list5, h)), COPY, scale=sb_t[:, t : t + 1])
-                nc.vector.tensor_tensor(diff[:, t, :], ga[:, t, :], gb[:, t, :], ALU.subtract)
+        def pick(h, t, ga, gb, diff):
+            nc.scalar.activation(ga, pw[t][:].indirect(half_of(list4, h)), COPY, scale=sa_t[:, t : t + 1])
+            nc.scalar.activation(gb, pv[t][:].indirect(half_of(list5, h)), COPY, scale=sb_t[:, t : t + 1])
+            nc.vector.tensor_tensor(diff[:, t, :], ga, gb, ALU.subtract)
+
+        def second_stage(h, diff):
             hid = sbuf([P, HALF, PACK], BF16, "hid%d" % h)
             woven = diff[:].rearrange("p t o -> p o t")
             nc.vector.scalar_tensor_tensor(hid[:], woven, -1.0, woven, ALU.mult, ALU.max)
@@ -178,17 +179,33 @@ def tile_list_twoownboards_twow_one_owntwopages_kernel(
                     start=True,
                     stop=True,
                 )
-            staged = sbuf([P, 2, HALF], F32, "p_sb%d" % h)
-            if h == 0:
-                nc.vector.tensor_copy(staged[:], acc_p[:])
-            else:
-                nc.scalar.copy(staged[:], acc_p[:])
-            p_sb.append(staged)
+            return acc_p
 
-        for h in range(2):
-            for g in range(2):
-                nc.scalar.activation(pa[g][:].indirect(half_of(list6, h)), p_sb[h][:, g, :], COPY)
-                nc.vector.tensor_copy(pb[g][:].indirect(half_of(list7, h)), p_sb[h][:, g, :])
+        def put_a(h, g):
+            nc.scalar.activation(pa[g][:].indirect(half_of(list6, h)), p_sb[h][:, g, :], COPY)
+
+        def put_b(h, g):
+            nc.vector.tensor_copy(pb[g][:].indirect(half_of(list7, h)), p_sb[h][:, g, :])
+
+        p_sb = [sbuf([P, 2, HALF], F32, "p_sb%d" % h) for h in range(2)]
+        diffs = [sbuf([P, PACK, HALF], F32, "diff0")]
+        picked0 = sbuf([P, PACK, 2, HALF], F32, "picked0", "b_sb2")
+        for t in range(PACK):
+            pick(0, t, picked0[:, t, 0, :], picked0[:, t, 1, :], diffs[0])
+        acc_p = second_stage(0, diffs[0])
+        diffs.append(sbuf([P, PACK, HALF], F32, "diff1", "hid_codes0"))
+        nc.vector.tensor_copy(p_sb[0][:], acc_p[:])
+        picked1 = sbuf([P, PACK, 2, HALF], F32, "picked1", "b_sb3")
+        for t in range(PACK):
+            pick(1, t, picked1[:, t, 0, :], picked1[:, t, 1, :], diffs[1])
+        put_a(0, 0)
+        put_a(0, 1)
+        for g in range(2):
+            nc.scalar.activation(pb[g][:].indirect(half_of(list7, 0)), p_sb[0][:, g, :], COPY)
+        nc.vector.tensor_copy(p_sb[1][:], second_stage(1, diffs[1])[:])
+        for g in range(2):
+            put_a(1, g)
+            put_b(1, g)
         for g in range(2):
             total = sbuf([P, E], F32, "total%d" % g)
             nc.vector.tensor_tensor(total[:], pa[g][:], pb[g][:], ALU.add)

@@ -54,10 +54,12 @@ def tile_list_twoownboards_twow_one_owntwopages_kernel(
         for plane in (x_plane, w_plane, w2_plane, wb_plane):
             nc.vector.memset(plane[:].bitcast(I32), 0)
 
-        x_rows = sbuf([4, 4, T // 4], I32, "x_rows")
-        nc.sync.dma_start(x_rows[:], xt_scales[0].bitcast(I32).rearrange("(q r) c -> r q c", r=4))
         w_rows = sbuf([4, 4, R // 4], I32, "w_rows")
         nc.sync.dma_start(w_rows[:], w_scales[0].bitcast(I32).rearrange("(q r) c -> r q c", r=4))
+        x_rows = sbuf([68, 2, T // 4], I32, "x_rows")
+        for u in range(2):
+            rows = xt_scales[0, 8 * u : 8 * u + 8, :].bitcast(I32).rearrange("(q r) c -> r q c", r=4)
+            nc.sync.dma_start(x_rows[64 * u : 64 * u + 4], rows)
         x_words = sbuf([P, T], U16, "x_words")
         nc.sync.dma_start(x_words[:].bitcast(I32), xt_words[0].bitcast(I32))
         list1 = load_list(offs, "list1")
@@ -81,17 +83,16 @@ def tile_list_twoownboards_twow_one_owntwopages_kernel(
         list4 = load_list(offs4, "list4")
 
         for q in range(4):
-            nc.vector.tensor_copy(x_plane[32 * q : 32 * q + 4, :].bitcast(I32), x_rows[:, q, :])
-        for q in range(4):
             nc.vector.tensor_copy(w_plane[32 * q : 32 * q + 4, :].bitcast(I32), w_rows[:, q, :])
         w_scale0 = sbuf([P, P], U8, "w_scale0")
         w_plane_dealt = w_plane[:].rearrange("p (m t) -> p t m", t=PACK)
         nc.vector.tensor_copy(w_scale0[:], w_plane_dealt[:, 0, :])
 
+        for q in range(4):
+            nc.vector.tensor_copy(x_plane[32 * q : 32 * q + 4, :].bitcast(I32), x_rows[64 * (q // 2) : 64 * (q // 2) + 4, q % 2, :])
         xg_words = sbuf([P, J], U16, "xg_words")
         xg_plane = sbuf([P, J], U8, "xg_plane")
         w_codes0 = sbuf([P, P], U32, "w_codes0")
-        w_codes = sbuf([P, PACK, P], U32, "w_codes")
 
         def gather_x(h):
             cols = slice(h * HALF, (h + 1) * HALF)
@@ -129,29 +130,38 @@ def tile_list_twoownboards_twow_one_owntwopages_kernel(
                 nc.vector.tensor_copy(staged[:, j0:j1], acc[:, 0 : j1 - j0])
             nc.scalar.activation(dest[:].indirect(lst[:, j0 // 16 : j1 // 16]), staged[:, j0:j1], COPY)
 
-        pw = [board("pw%d" % t) for t in range(PACK)]
+        pw = [board("pw0"), board("pw1")]
         gather_x(0)
         w_raw_dealt = w_raw[:].bitcast(U32).rearrange("p (m t) -> p t m", t=PACK)
         nc.scalar.copy(w_codes0[:], w_raw_dealt[:, 0, :])
-        nc.scalar.copy(w_codes[:, 1:PACK, :], w_raw_dealt[:, 1:PACK, :])
+        w_codes1 = sbuf([P, P], U32, "w_codes1")
+        nc.scalar.copy(w_codes1[:], w_raw_dealt[:, 1, :])
         gather_x(1)
         put_first(first_product(w_codes0[:], w_scale0[:], E4M3, 0, HALF), a_sb[0], pw[0], list2, 0, HALF)
         put_first(first_product(w_codes0[:], w_scale0[:], E4M3, HALF, J), a_sb[0], pw[0], list2, HALF, J)
-        w_scale = sbuf([P, PACK, P], U8, "w_scale", "x_words")
-        for t in range(1, PACK):
+        w_scale1 = sbuf([P, P], U8, "w_scale1", "x_words")
+        nc.vector.tensor_copy(w_scale1[:], w_plane_dealt[:, 1, :])
+        accs = {1: first_product(w_codes1[:], w_scale1[:], E4M3, 0, J)}
+        w_scale = sbuf([P, PACK, P], U8, "w_scale", "x_plane")
+        w_codes = sbuf([P, PACK, P], I32, "w_codes", "w_codes0")
+        for t in range(2, PACK):
             nc.vector.tensor_copy(w_scale[:, t, :], w_plane_dealt[:, t, :])
-        accs = {t: first_product(w_codes[:, t, :], w_scale[:, t, :], E4M3, 0, J) for t in range(1, PACK)}
+            deal(w_codes, w_raw, t)
+        for t in range(2, PACK):
+            accs[t] = first_product(w_codes[:, t, :], w_scale[:, t, :], E4M3, 0, J)
         for t in range(1, PACK):
+            if t >= 2:
+                pw.append(board("pw%d" % t, ("w_plane", "w_raw")[t - 2]))
             put_first(accs[t], a_sb[t], pw[t], list2, 0, J)
-        w2_codes = sbuf([P, PACK, P], I32, "w2_codes", "w_codes")
-        w2_scale = sbuf([P, PACK, P], U8, "w2_scale", "x_words")
+        w2_codes = sbuf([P, PACK, P], I32, "w2_codes", "w_codes0")
+        w2_scale = sbuf([P, PACK, P], U8, "w2_scale", "x_plane")
         nc.vector.tensor_copy(w2_scale[:], w2_plane[:].rearrange("p (m t) -> p t m", t=PACK))
         for t in range(PACK):
             deal(w2_codes, w2_raw, t)
         accs = {t: first_product(w2_codes[:, t, :], w2_scale[:, t, :], E5M2, 0, J) for t in range(PACK)}
         pv = []
         for t in range(PACK):
-            pv.append(board("pv%d" % t, ("w2_plane", "w2_raw", "w_codes", "x_words")[t]))
+            pv.append(board("pv%d" % t, ("w2_plane", "w2_raw", "w_codes0", "x_plane")[t]))
             put_first(accs[t], b_sb[t], pv[t], list3, 0, J)
         pa = [board("pa0", "xg_words"), board("pa1", "xg_plane")]
         pb = [board("pb0", "b_sb0"), board("pb1", "b_sb1")]
@@ -207,6 +217,8 @@ def tile_list_twoownboards_twow_one_owntwopages_kernel(
             put_a(1, g)
             put_b(1, g)
         for g in range(2):
-            total = sbuf([P, E], F32, "total%d" % g)
-            nc.vector.tensor_tensor(total[:], pa[g][:], pb[g][:], ALU.add)
-            nc.sync.dma_start(out[P * g : P * (g + 1), :], total[:])
+            for e0, e1 in ((0, E),) if g == 0 else ((0, E // 2), (E // 2, E)):
+                total = sbuf([P, e1 - e0], F32, "total%d_%d" % (g, e0))
+                nc.vector.tensor_tensor(total[:], pa[g][:, e0:e1], pb[g][:, e0:e1], ALU.add)
+                queue = nc.scalar if e0 else nc.sync
+                queue.dma_start(out[P * g : P * (g + 1), e0:e1], total[:])

from contextlib import ExitStack

import concourse.mybir as mybir

K, T, J, R, C, O, N, E = 512, 1024, 256, 512, 512, 256, 256, 512
FLOPS = 2 * K * R * J * 2 + 2 * R * N * O

F32 = mybir.dt.float32
BF16 = mybir.dt.bfloat16
I32 = mybir.dt.int32
U32 = mybir.dt.uint32
U16 = mybir.dt.uint16
U8 = mybir.dt.uint8
E4M3 = mybir.dt.float8_e4m3fn_x4
E5M2 = mybir.dt.float8_e5m2_x4
E2M1 = mybir.dt.float4_e2m1fn_x4
ALU = mybir.AluOpType
COPY = mybir.ActivationFunctionType.Copy

P = 128
PACK = 4
HALF = 128


def tile_list_twoownboards_twow_one_owntwopages_kernel(
    tc, xt_words, xt_scales, w_words, w_scales, w2_words, w2_scales, sa, sb, wb_words, wb_scales,
    offs, offs2, offs3, offs4, offs5, offs6, offs7, out
):
    nc = tc.nc
    with ExitStack() as ctx:
        held = ctx.enter_context(tc.tile_pool(name="held", bufs=1))
        psum_ab = ctx.enter_context(tc.psum_pool(name="psum_ab", bufs=6))
        psum_p = ctx.enter_context(tc.psum_pool(name="psum_p", bufs=2))

        def sbuf(shape, dtype, name, tag=None):
            return held.tile(shape, dtype, name=name, tag=tag or name, align_bytes=64)

        def load_list(src, name):
            lst = held.tile([P, J // 16], U16, name=name)
            nc.sync.dma_start(lst[:], src)
            return lst

        def load_plane(plane, scales):
            for q in range(4):
                nc.sync.dma_start(plane[32 * q : 32 * q + 4, :].bitcast(I32), scales[0, 4 * q : 4 * q + 4, :].bitcast(I32))

        def half_of(lst, h):
            return lst[:, h * HALF // 16 : (h + 1) * HALF // 16]

        x_plane = sbuf([P, T], U8, "x_plane")
        w_plane = sbuf([P, R], U8, "w_plane")
        w2_plane = sbuf([P, R], U8, "w2_plane")
        wb_plane = sbuf([P, N], U8, "wb_plane")
        for plane in (x_plane, w_plane, w2_plane, wb_plane):
            nc.vector.memset(plane[:].bitcast(I32), 0)

        w_rows = sbuf([4, 4, R // 4], I32, "w_rows")
        nc.sync.dma_start(w_rows[:], w_scales[0].bitcast(I32).rearrange("(q r) c -> r q c", r=4))
        x_rows = sbuf([68, 2, T // 4], I32, "x_rows")
        for u in range(2):
            rows = xt_scales[0, 8 * u : 8 * u + 8, :].bitcast(I32).rearrange("(q r) c -> r q c", r=4)
            nc.sync.dma_start(x_rows[64 * u : 64 * u + 4], rows)
        x_words = sbuf([P, T], U16, "x_words")
        nc.sync.dma_start(x_words[:].bitcast(I32), xt_words[0].bitcast(I32))
        list1 = load_list(offs, "list1")
        w_raw = sbuf([P, R], I32, "w_raw")
        nc.sync.dma_start(w_raw[:], w_words[0].rearrange("p n t -> p (n t)").bitcast(I32))
        list2 = load_list(offs2, "list2")
        w2_raw = sbuf([P, R], I32, "w2_raw")
        nc.sync.dma_start(w2_raw[:], w2_words[0].rearrange("p n t -> p (n t)").bitcast(I32))
        load_plane(w2_plane, w2_scales)
        list3 = load_list(offs3, "list3")
        wb_codes = sbuf([P, 2 * N], U8, "wb_codes")
        nc.sync.dma_start(wb_codes[:].bitcast(I32), wb_words[0].bitcast(I32))
        load_plane(wb_plane, wb_scales)
        list6 = load_list(offs6, "list6")
        list7 = load_list(offs7, "list7")
        sa_t = sbuf([P, PACK], F32, "sa_t")
        nc.sync.dma_start(sa_t[:], sa.rearrange("(p t) o -> p (t o)", t=PACK))
        sb_t = sbuf([P, PACK], F32, "sb_t")
        nc.sync.dma_start(sb_t[:], sb.rearrange("(p t) o -> p (t o)", t=PACK))
        list5 = load_list(offs5, "list5")
        list4 = load_list(offs4, "list4")

        for q in range(4):
            nc.vector.tensor_copy(w_plane[32 * q : 32 * q + 4, :].bitcast(I32), w_rows[:, q, :])
        w_scale0 = sbuf([P, P], U8, "w_scale0")
        w_plane_dealt = w_plane[:].rearrange("p (m t) -> p t m", t=PACK)
        nc.vector.tensor_copy(w_scale0[:], w_plane_dealt[:, 0, :])

        for q in range(4):
            nc.vector.tensor_copy(x_plane[32 * q : 32 * q + 4, :].bitcast(I32), x_rows[64 * (q // 2) : 64 * (q // 2) + 4, q % 2, :])
        xg_words = sbuf([P, J], U16, "xg_words")
        xg_plane = sbuf([P, J], U8, "xg_plane")
        w_codes0 = sbuf([P, P], U32, "w_codes0")

        def gather_x(h):
            cols = slice(h * HALF, (h + 1) * HALF)
            nc.vector.tensor_copy(xg_words[:, cols], x_words[:].indirect(half_of(list1, h)))
            nc.vector.tensor_copy(xg_plane[:, cols], x_plane[:].indirect(half_of(list1, h)))

        def deal(codes, raw, t):
            nc.vector.tensor_copy(codes[:, t, :], raw[:].rearrange("p (m t) -> p t m", t=PACK)[:, t, :])

        def board(name, tag=None):
            tile_ = sbuf([P, C], F32, name, tag)
            nc.vector.memset(tile_[:], 0.0)
            return tile_

        a_sb = [sbuf([P, J], F32, "a_sb%d" % t) for t in range(PACK)]
        b_sb = [sbuf([P, J], F32, "b_sb%d" % t) for t in range(PACK)]

        def first_product(codes, scale, fmt, j0, j1):
            acc = psum_ab.tile([P, J], F32, name="acc")
            nc.tensor.matmul_mx(
                out=acc[:, 0 : j1 - j0],
                lhsT=codes.bitcast(fmt),
                lhsT_scale=scale,
                rhs=xg_words[:, j0:j1].bitcast(E2M1),
                rhs_scale=xg_plane[:, j0:j1],
                start=True,
                stop=True,
            )
            return acc

        def put_first(acc, staged, dest, lst, j0, j1):
            if j1 == HALF:
                nc.scalar.copy(staged[:, j0:j1], acc[:, 0 : j1 - j0])
            else:
                nc.vector.tensor_copy(staged[:, j0:j1], acc[:, 0 : j1 - j0])
            nc.scalar.activation(dest[:].indirect(lst[:, j0 // 16 : j1 // 16]), staged[:, j0:j1], COPY)

        pw = [board("pw0"), board("pw1")]
        gather_x(0)
        w_raw_dealt = w_raw[:].bitcast(U32).rearrange("p (m t) -> p t m", t=PACK)
        nc.scalar.copy(w_codes0[:], w_raw_dealt[:, 0, :])
        w_codes1 = sbuf([P, P], U32, "w_codes1")
        nc.scalar.copy(w_codes1[:], w_raw_dealt[:, 1, :])
        gather_x(1)
        put_first(first_product(w_codes0[:], w_scale0[:], E4M3, 0, HALF), a_sb[0], pw[0], list2, 0, HALF)
        put_first(first_product(w_codes0[:], w_scale0[:], E4M3, HALF, J), a_sb[0], pw[0], list2, HALF, J)
        w_scale1 = sbuf([P, P], U8, "w_scale1", "x_words")
        nc.vector.tensor_copy(w_scale1[:], w_plane_dealt[:, 1, :])
        accs = {1: first_product(w_codes1[:], w_scale1[:], E4M3, 0, J)}
        w_scale = sbuf([P, PACK, P], U8, "w_scale", "x_plane")
        w_codes = sbuf([P, PACK, P], I32, "w_codes", "w_codes0")
        for t in range(2, PACK):
            nc.vector.tensor_copy(w_scale[:, t, :], w_plane_dealt[:, t, :])
            deal(w_codes, w_raw, t)
        for t in range(2, PACK):
            accs[t] = first_product(w_codes[:, t, :], w_scale[:, t, :], E4M3, 0, J)
        for t in range(1, PACK):
            if t >= 2:
                pw.append(board("pw%d" % t, ("w_plane", "w_raw")[t - 2]))
            put_first(accs[t], a_sb[t], pw[t], list2, 0, J)
        w2_codes = sbuf([P, PACK, P], I32, "w2_codes", "w_codes0")
        w2_scale = sbuf([P, PACK, P], U8, "w2_scale", "x_plane")
        nc.vector.tensor_copy(w2_scale[:], w2_plane[:].rearrange("p (m t) -> p t m", t=PACK))
        for t in range(PACK):
            deal(w2_codes, w2_raw, t)
        accs = {t: first_product(w2_codes[:, t, :], w2_scale[:, t, :], E5M2, 0, J) for t in range(PACK)}
        pv = []
        for t in range(PACK):
            pv.append(board("pv%d" % t, ("w2_plane", "w2_raw", "w_codes0", "x_plane")[t]))
            put_first(accs[t], b_sb[t], pv[t], list3, 0, J)
        pa = [board("pa0", "xg_words"), board("pa1", "xg_plane")]
        pb = [board("pb0", "b_sb0"), board("pb1", "b_sb1")]

        def pick(h, t, ga, gb, diff):
            nc.scalar.activation(ga, pw[t][:].indirect(half_of(list4, h)), COPY, scale=sa_t[:, t : t + 1])
            nc.scalar.activation(gb, pv[t][:].indirect(half_of(list5, h)), COPY, scale=sb_t[:, t : t + 1])
            nc.vector.tensor_tensor(diff[:, t, :], ga, gb, ALU.subtract)

        def second_stage(h, diff):
            hid = sbuf([P, HALF, PACK], BF16, "hid%d" % h)
            woven = diff[:].rearrange("p t o -> p o t")
            nc.vector.scalar_tensor_tensor(hid[:], woven, -1.0, woven, ALU.mult, ALU.max)
            hid_codes = sbuf([P, HALF], I32, "hid_codes%d" % h)
            hid_scale = sbuf([P, HALF], U8, "hid_scale%d" % h)
            nc.vector.quantize_mx(hid_codes[:].bitcast(E5M2), hid_scale[:], hid[:].rearrange("p o t -> p (o t)"))
            acc_p = psum_p.tile([P, 2, HALF], F32, name="acc_p")
            for g in range(2):
                nc.tensor.matmul_mx(
                    out=acc_p[:, g, :],
                    lhsT=wb_codes[:, 2 * P * g : 2 * P * (g + 1)].bitcast(E2M1),
                    lhsT_scale=wb_plane[:, P * g : P * (g + 1)],
                    rhs=hid_codes[:].bitcast(E5M2),
                    rhs_scale=hid_scale[:],
                    start=True,
                    stop=True,
                )
            return acc_p

        def put_a(h, g):
            nc.scalar.activation(pa[g][:].indirect(half_of(list6, h)), p_sb[h][:, g, :], COPY)

        def put_b(h, g):
            nc.vector.tensor_copy(pb[g][:].indirect(half_of(list7, h)), p_sb[h][:, g, :])

        p_sb = [sbuf([P, 2, HALF], F32, "p_sb%d" % h) for h in range(2)]
        diffs = [sbuf([P, PACK, HALF], F32, "diff0")]
        picked0 = sbuf([P, PACK, 2, HALF], F32, "picked0", "b_sb2")
        for t in range(PACK):
            pick(0, t, picked0[:, t, 0, :], picked0[:, t, 1, :], diffs[0])
        acc_p = second_stage(0, diffs[0])
        diffs.append(sbuf([P, PACK, HALF], F32, "diff1", "hid_codes0"))
        nc.vector.tensor_copy(p_sb[0][:], acc_p[:])
        picked1 = sbuf([P, PACK, 2, HALF], F32, "picked1", "b_sb3")
        for t in range(PACK):
            pick(1, t, picked1[:, t, 0, :], picked1[:, t, 1, :], diffs[1])
        put_a(0, 0)
        put_a(0, 1)
        for g in range(2):
            nc.scalar.activation(pb[g][:].indirect(half_of(list7, 0)), p_sb[0][:, g, :], COPY)
        nc.vector.tensor_copy(p_sb[1][:], second_stage(1, diffs[1])[:])
        for g in range(2):
            put_a(1, g)
            put_b(1, g)
        for g in range(2):
            for e0, e1 in ((0, E),) if g == 0 else ((0, E // 2), (E // 2, E)):
                total = sbuf([P, e1 - e0], F32, "total%d_%d" % (g, e0))
                nc.vector.tensor_tensor(total[:], pa[g][:, e0:e1], pb[g][:, e0:e1], ALU.add)
                queue = nc.scalar if e0 else nc.sync
                queue.dma_start(out[P * g : P * (g + 1), e0:e1], total[:])
